import numpy as np
import ml_dtypes


def mxq(x, axis, fmt="e4m3"):
    dtype, down = {"e4m3": (ml_dtypes.float8_e4m3fn, 7), "e5m2": (ml_dtypes.float8_e5m2, 14)}[fmt]
    v = np.moveaxis(np.asarray(x, np.float32).astype(ml_dtypes.bfloat16).astype(np.float64), axis, -1)
    blocks = v.reshape(v.shape[:-1] + (-1, 32))
    amax = np.abs(blocks).max(-1, keepdims=True)
    byte = np.maximum(np.where(amax > 0, np.frexp(amax)[1] - 1 + 127, 0) - down, 1)
    scale = np.exp2(byte - 127.0)
    codes = (blocks / scale).astype(np.float32).astype(dtype).astype(np.float64)
    return np.moveaxis((codes * scale).reshape(v.shape), -1, axis)


WIDE = False


def mx_kscale(k):
    if not WIDE:
        return np.ones(k)
    levels = np.array([10, -10, 5, -5, 0])
    if k % 512:
        return np.exp2(np.random.permutation(np.resize(levels, k // 32))).repeat(32)
    a = np.empty((k // 512, 16))
    for p in range(k // 512):
        a[p, :8] = np.random.permutation(np.resize(levels, 8))
        for g in range(8):
            far = levels[np.abs(levels - a[p, g]) >= 10]
            a[p, g + 8] = far[np.random.randint(len(far))]
    return np.exp2(a.ravel()).repeat(32)


def f64(x):
    return np.asarray(x).astype(np.float64)


def striped8(idx):
    return np.asarray(idx).reshape(8, -1, 16).transpose(0, 2, 1).reshape(128, -1).astype(np.uint16)


def unstriped8(offs):
    return offs.reshape(8, 16, -1).transpose(0, 2, 1).reshape(8, -1).astype(np.int64)


def pick8(x, idx, run):
    r = np.arange(len(x))
    return x[r[:, None], idx[r % (8 * run) // run]]


E2M1 = np.array([0.0, 0.5, 1.0, 1.5, 2.0, 3.0, 4.0, 6.0, -0.0, -0.5, -1.0, -1.5, -2.0, -3.0, -4.0, -6.0])


def pack_weight(w, fmt):
    k, n = w.shape
    w = f64(np.asarray(w, np.float32).astype(ml_dtypes.bfloat16)).reshape(k // 32, 32, n)
    amax = np.abs(w).max(1)
    if fmt == "e4m3":
        byte = np.frexp(amax)[1] - 1 + 127 - 7
    else:
        mant, ex = np.frexp(amax / 6.0)
        byte = np.where(mant > 0.5, ex, ex - 1) + 127
    byte = np.clip(np.where(amax > 0, byte, 1), 1, 254)
    scaled = (w * np.exp2(127.0 - byte)[:, None, :]).reshape(k, n).astype(np.float32)
    by_word = np.ascontiguousarray(scaled.reshape(k // 512, 128, 4, n).transpose(0, 1, 3, 2))
    if fmt == "e4m3":
        words = by_word.astype(ml_dtypes.float8_e4m3fn).view(np.uint8)
    else:
        c = by_word.astype(ml_dtypes.float4_e2m1fn).view(np.uint8) & 0xF
        words = (c[..., 0::2] | (c[..., 1::2] << 4)).reshape(k // 512, 128, 2 * n)
    return np.ascontiguousarray(words), np.ascontiguousarray(byte.astype(np.uint8).reshape(k // 512, 16, n))


def unpack_weight(words, scales, fmt):
    g, _, n = scales.shape
    words = np.ascontiguousarray(words).reshape(g, 128, n, -1)
    if fmt == "e4m3":
        vals = words.view(ml_dtypes.float8_e4m3fn).astype(np.float64)
    else:
        nib = np.empty((g, 128, n, 4), np.uint8)
        nib[..., 0::2] = words & 0xF
        nib[..., 1::2] = words >> 4
        vals = E2M1[nib]
    vals = vals * np.repeat(np.exp2(scales.astype(np.float64) - 127.0), 8, axis=1)[..., None]
    return vals.transpose(0, 1, 3, 2).reshape(g * 512, n)


def sigmoid(v):
    return 1.0 / (1.0 + np.exp(-v))


D, V, Q, I = 512, 2048, 128, 512


def setup_inputs():
    n = np.random.standard_normal
    idx = np.stack([np.random.permutation(V)[:I] for _ in range(8)])
    idx2 = np.stack([np.random.permutation(V)[:I] for _ in range(8)])
    fd = mx_kscale(D)
    vocp = pack_weight(n((D, V)) / fd[:, None], "e4m3")
    return {
        "hid": (n((D, Q)) * 1.0 / np.sqrt(D) * fd[:, None]).astype(np.float32),
        "voc_words": vocp[0],
        "voc_scales": vocp[1],
        "sw": (np.random.uniform(0.5, 2.0, (1, I))).astype(np.float32),
        "sw2": (np.random.uniform(0.5, 2.0, (1, I))).astype(np.float32),
        "saved": (np.random.uniform(-0.5, 0.5, (Q, 1))).astype(np.float32),
        "beta": (np.random.uniform(1.0, 3.0, (Q, 1))).astype(np.float32),
        "old": (0.5 * n((Q, V))).astype(np.float32),
        "offs": striped8(idx),
        "offs2": striped8(idx2),
    }


def reference(hid, voc_words, voc_scales, sw, sw2, saved, beta, old, offs, offs2):
    idx = unstriped8(offs)
    idx2 = unstriped8(offs2)
    vocu = unpack_weight(voc_words, voc_scales, "e4m3")
    hidq = mxq(f64(hid), 0, "e4m3")
    a = hidq.T @ vocu
    m1 = np.max(a, axis=1, keepdims=True)
    px = np.exp(pick8(a, idx, 16) - m1)
    px2 = np.exp(pick8(a, idx2, 16) - m1)
    s1l = np.sum(px * f64(sw), axis=1, keepdims=True)
    s2l = np.sum(px2 * f64(sw2), axis=1, keepdims=True)
    dl = np.log(s1l) - np.log(s2l) - f64(saved)
    ddl = sigmoid(dl * f64(beta) * (-1.0)) * f64(beta)
    ds2l = ddl * (-1.0) / s2l
    ds1l = ddl / s1l
    dpx2 = ds2l * f64(sw2)
    dpx = ds1l * f64(sw)
    e1 = dpx2 * px2
    s1 = np.zeros((Q, V))
    s1[np.arange(Q)[:, None], idx2[np.arange(Q) % 128 // 16]] = e1
    e2 = dpx * px
    s2 = np.zeros((Q, V))
    s2[np.arange(Q)[:, None], idx[np.arange(Q) % 128 // 16]] = e2
    da = s1 + s2
    y = da * 256.0 + f64(old)
    return y

@@ -1,0 +1,189 @@
+from contextlib import ExitStack
+
+import concourse.mybir as mybir
+from concourse.masks import make_identity
+
+D, V, Q, I = 512, 2048, 128, 512
+FLOPS = 2 * D * V * Q
+
+F32 = mybir.dt.float32
+BF16 = mybir.dt.bfloat16
+I32 = mybir.dt.int32
+U32 = mybir.dt.uint32
+U16 = mybir.dt.uint16
+U8 = mybir.dt.uint8
+FP8X4 = mybir.dt.float8_e4m3fn_x4
+ALU = mybir.AluOpType
+ACT = mybir.ActivationFunctionType
+AX = mybir.AxisListType
+
+P = 128
+BANK = 512
+SCORE_PIECES = [(0, 256), (256, 256), (512, 512), (1024, 512), (1536, 512)]
+DIRECT = 256
+TURNED = [(256, 256), (512, 512), (1024, 512), (1536, 512)]
+OUT_PIECES = [(0, 256), (256, 256), (512, 512), (1024, 512), (1536, 256), (1792, 256)]
+
+
+def tile_attend_bodds_heads_kernel(tc, hid, voc_words, voc_scales, sw, sw2, saved, beta, old, offs, offs2, out):
+    nc = tc.nc
+    with ExitStack() as ctx:
+        keep = ctx.enter_context(tc.tile_pool(name="keep", bufs=1))
+        psum = ctx.enter_context(tc.psum_pool(name="psum", bufs=1))
+
+        planes = keep.tile([P, BANK], U8, name="planes", align_bytes=64)
+        nc.gpsimd.memset(planes[:].bitcast(I32), 0)
+        hid_raw = keep.tile([P, 4, Q], F32, name="hid_raw")
+        nc.sync.dma_start(out=hid_raw[:], in_=hid.rearrange("(p t) q -> p t q", t=4))
+        for quad in range(4):
+            nc.sync.dma_start(
+                out=planes[32 * quad : 32 * quad + 16, :].bitcast(I32),
+                in_=voc_scales[0, 4 * quad : 4 * quad + 4, :].bitcast(I32).rearrange("r (j c) -> j r c", j=4),
+            )
+        words_hbm = voc_words[0].rearrange("p n t -> p (n t)").bitcast(I32)
+        words = []
+        for j, (c0, n) in enumerate(SCORE_PIECES):
+            w = keep.tile([P, n], U32, name=f"words{j}", align_bytes=64)
+            nc.sync.dma_start(out=w[:].bitcast(I32), in_=words_hbm[:, c0 : c0 + n])
+            words.append(w)
+        list1 = keep.tile([P, I // 16], U16, name="list1")
+        nc.sync.dma_start(list1[:], offs)
+        list2 = keep.tile([P, I // 16], U16, name="list2")
+        nc.sync.dma_start(list2[:], offs2)
+        sw1_t = keep.tile([P, I], F32, name="sw1_t")
+        sw2_t = keep.tile([P, I], F32, name="sw2_t")
+        nc.sync.dma_start(out=sw2_t[:], in_=sw2[0].partition_broadcast(P))
+        nc.sync.dma_start(out=sw1_t[:], in_=sw[0].partition_broadcast(P))
+        beta_t = keep.tile([P, 1], F32, name="beta_t")
+        saved_t = keep.tile([P, 1], F32, name="saved_t")
+        nc.sync.dma_start(out=beta_t[:], in_=beta)
+        nc.sync.dma_start(out=saved_t[:], in_=saved)
+        old_t = []
+        for b in range(V // BANK):
+            o = keep.tile([P, BANK], F32, name=f"old{b}", tag=f"old_then_scaled{b}")
+            nc.sync.dma_start(out=o[:], in_=old[:, b * BANK : (b + 1) * BANK])
+            old_t.append(o)
+
+        win2 = keep.tile([P, V], F32, name="win2")
+        nc.vector.memset(win2[:], 0.0)
+        ident = keep.tile([P, P], F32, name="ident")
+        make_identity(nc, ident[:])
+
+
+        hid_bf = keep.tile([P, Q, 4], BF16, name="hid_bf", tag="hid_bf_then_win1", align_bytes=64)
+        nc.vector.tensor_copy(out=hid_bf[:], in_=hid_raw[:].rearrange("p t q -> p q t"))
+        hid_codes = keep.tile([P, Q], U32, name="hid_codes", align_bytes=64)
+        hid_scales = keep.tile([P, Q], U8, name="hid_scales", align_bytes=64)
+        nc.vector.quantize_mx(out=hid_codes[:].bitcast(FP8X4), scales=hid_scales[:], in_=hid_bf[:].rearrange("p q t -> p (q t)"))
+        win1 = keep.tile([P, V], F32, name="win1", tag="hid_bf_then_win1", align_bytes=64)
+        nc.gpsimd.memset(win1[:], 0.0)
+
+        a = keep.tile([P, V], F32, name="a")
+        piece_max = keep.tile([P, 8], F32, name="piece_max")
+        early_max = keep.tile([P, 1], F32, name="early_max")
+        row_max = keep.tile([P, 1], F32, name="row_max")
+        last = len(SCORE_PIECES) - 1
+        for j, (c0, n) in enumerate(SCORE_PIECES):
+            bank = psum.tile([P, BANK], F32, name=f"score{j}", tag=f"bank{j}")
+            k = 4 * (c0 // BANK)
+            nc.tensor.matmul_mx(
+                out=bank[:, 0:n],
+                lhsT=hid_codes[:].bitcast(FP8X4),
+                lhsT_scale=hid_scales[:],
+                rhs=words[j][:].bitcast(FP8X4),
+                rhs_scale=planes[k:P, c0 % BANK : c0 % BANK + n],
+                start=True,
+                stop=True,
+            )
+            if j < last:
+                nc.vector.tensor_scalar(out=a[:, c0 : c0 + n], in0=bank[:, 0:n], scalar1=1.0, scalar2=None, op0=ALU.mult, op1=ALU.max, accum_out=piece_max[:, j : j + 1])
+            else:
+                nc.vector.tensor_reduce(out=early_max[:], in_=piece_max[:, 0:last], axis=AX.X, op=ALU.max)
+                nc.vector.tensor_scalar(out=a[:, c0 : c0 + n], in0=bank[:, 0:n], scalar1=1.0, scalar2=early_max[:], op0=ALU.mult, op1=ALU.max, accum_out=row_max[:])
+        neg_max = keep.tile([P, 1], F32, name="neg_max")
+        nc.scalar.activation(out=neg_max[:], in_=row_max[:], func=ACT.Copy, scale=-1.0)
+
+        neg_beta = keep.tile([P, 1], F32, name="neg_beta")
+        beta_saved = keep.tile([P, 1], F32, name="beta_saved")
+        beta256 = keep.tile([P, 2], F32, name="beta256")
+        nc.scalar.activation(out=neg_beta[:], in_=beta_t[:], func=ACT.Copy, scale=-1.0)
+        nc.scalar.activation(out=beta_saved[:], in_=saved_t[:], func=ACT.Copy, scale=beta_t[:])
+        nc.scalar.activation(out=beta256[:, 0:1], in_=beta_t[:], func=ACT.Copy, scale=256.0)
+        nc.scalar.activation(out=beta256[:, 1:2], in_=beta_t[:], func=ACT.Copy, scale=-256.0)
+
+        nturn = len(TURNED)
+        turned = []
+        for b, (c0, n) in enumerate(TURNED):
+            t = psum.tile([P, BANK], F32, name=f"turned{b}", tag=f"bank{(5 + b) % 8}")
+            turned.append(t)
+            src = old_t[c0 // BANK]
+            for i in range(n // P):
+                o = c0 % BANK + i * P
+                nc.tensor.matmul(t[:, i * P : (i + 1) * P], lhsT=src[:, o : o + P], rhs=ident[:], start=(i == 0), stop=False, is_transpose=True)
+
+        px2 = keep.tile([P, I], F32, name="px2")
+        g2 = keep.tile([P, I], F32, name="g2")
+        nc.vector.tensor_copy(out=g2[:], in_=a[:].indirect(list2[:]))
+        nc.scalar.activation(out=px2[:], in_=g2[:], func=ACT.Exp, bias=neg_max[:])
+        g1 = keep.tile([P, I], F32, name="g1")
+        nc.vector.tensor_copy(out=g1[:], in_=a[:].indirect(list1[:]))
+        px1 = keep.tile([P, I], F32, name="px1")
+        nc.scalar.activation(out=px1[:], in_=g1[:], func=ACT.Exp, bias=neg_max[:])
+        sum1 = keep.tile([P, 1], F32, name="sum1")
+        sum2 = keep.tile([P, 1], F32, name="sum2")
+        w1 = keep.tile([P, I], F32, name="w1")
+        w2 = keep.tile([P, I], F32, name="w2")
+        inv1 = keep.tile([P, 1], F32, name="inv1")
+        inv2 = keep.tile([P, 1], F32, name="inv2")
+        nc.vector.scalar_tensor_tensor(out=w2[:], in0=px2[:], scalar=1.0, in1=sw2_t[:], op0=ALU.mult, op1=ALU.mult, accum_out=sum2[:])
+        nc.vector.scalar_tensor_tensor(out=w1[:], in0=px1[:], scalar=1.0, in1=sw1_t[:], op0=ALU.mult, op1=ALU.mult, accum_out=sum1[:])
+        nc.vector.reciprocal(out=inv2[:], in_=sum2[:])
+        nc.vector.tensor_copy(out=win2[:].indirect(list2[:]), in_=w2[:])
+        nc.vector.reciprocal(out=inv1[:], in_=sum1[:])
+        nc.vector.tensor_copy(out=win1[:].indirect(list1[:]), in_=w1[:])
+
+        log_odds = keep.tile([P, 1], F32, name="log_odds")
+        nc.scalar.activation(out=log_odds[:], in_=sum1[:], func=ACT.Ln, scale=inv2[:])
+        pre2 = keep.tile([P, 1], F32, name="pre2")
+        nc.scalar.activation(out=pre2[:], in_=inv2[:], func=ACT.Copy, scale=beta256[:, 1:2])
+        sig = keep.tile([P, 1], F32, name="sig")
+        nc.scalar.activation(out=sig[:], in_=log_odds[:], func=ACT.Sigmoid, scale=neg_beta[:], bias=beta_saved[:])
+        coef2 = keep.tile([P, 1], F32, name="coef2")
+        nc.scalar.activation(out=coef2[:], in_=pre2[:], func=ACT.Copy, scale=sig[:])
+        coef1 = keep.tile([P, 1], F32, name="coef1")
+        nc.vector.tensor_scalar(out=coef1[:], in0=inv1[:], scalar1=sig[:], scalar2=beta256[:, 0:1], op0=ALU.mult, op1=ALU.mult)
+
+        scaled = [keep.tile([P, BANK], F32, name=f"scaled{b}", tag=f"old_then_scaled{(3, 2, 1, 4)[b]}") for b in range(nturn)]
+        summed = [keep.tile([P, BANK], F32, name=f"summed{b}") for b in range(nturn)]
+        back = [psum.tile([P, BANK], F32, name=f"back{b}", tag=f"bank{b + 1}") for b in range(nturn)]
+
+        def scale_and_add(b):
+            c0, n = TURNED[b]
+            nc.scalar.activation(out=scaled[b][:, 0:n], in_=win2[:, c0 : c0 + n], func=ACT.Copy, scale=coef2[:])
+            for i in range(n // P):
+                nc.tensor.matmul(turned[b][:, i * P : (i + 1) * P], lhsT=scaled[b][:, i * P : (i + 1) * P], rhs=ident[:], start=False, stop=(i == n // P - 1), is_transpose=True)
+
+        def turn_back(b):
+            c0, n = TURNED[b]
+            nc.scalar.copy(out=summed[b][:, 0:n], in_=turned[b][:, 0:n])
+            for i in range(n // P):
+                nc.tensor.transpose(back[b][:, i * P : (i + 1) * P], summed[b][:, i * P : (i + 1) * P], ident[:])
+
+        scale_and_add(0)
+        for b in range(nturn):
+            if b + 1 < nturn:
+                scale_and_add(b + 1)
+            turn_back(b)
+
+        part = keep.tile([P, DIRECT], F32, name="part")
+        nc.vector.scalar_tensor_tensor(out=part[:], in0=win2[:, 0:DIRECT], scalar=coef2[:], in1=old_t[0][:, 0:DIRECT], op0=ALU.mult, op1=ALU.add)
+        for j, (c0, n) in enumerate(OUT_PIECES):
+            res = keep.tile([P, n], F32, name=f"res{j}")
+            if c0 < DIRECT:
+                other = part[:, c0 : c0 + n]
+            else:
+                b = c0 // BANK
+                off = c0 - TURNED[b][0]
+                other = back[b][:, off : off + n]
+            nc.vector.scalar_tensor_tensor(out=res[:], in0=win1[:, c0 : c0 + n], scalar=coef1[:], in1=other, op0=ALU.mult, op1=ALU.add)
+            nc.sync.dma_start(out=out[:, c0 : c0 + n], in_=res[:])

@@ -20,9 +20,9 @@ AX = mybir.AxisListType
 P = 128
 BANK = 512
 SCORE_PIECES = [(0, 256), (256, 256), (512, 512), (1024, 512), (1536, 512)]
-DIRECT = 256
-TURNED = [(256, 256), (512, 512), (1024, 512), (1536, 512)]
-OUT_PIECES = [(0, 256), (256, 256), (512, 512), (1024, 512), (1536, 256), (1792, 256)]
+DIRECT = 384
+TURNED = [(0, 512), (512, 512), (1024, 512), (1536, 128)]
+OUT_PIECES = [(V - DIRECT, DIRECT)] + TURNED
 
 
 def tile_attend_bodds_heads_kernel(tc, hid, voc_words, voc_scales, sw, sw2, saved, beta, old, offs, offs2, out):
@@ -42,18 +42,18 @@ def tile_attend_bodds_heads_kernel(tc, hid, voc_words, voc_scales, sw, sw2, save
             )
         words_hbm = voc_words[0].rearrange("p n t -> p (n t)").bitcast(I32)
         words = []
-        for j, (c0, n) in enumerate(SCORE_PIECES):
-            w = keep.tile([P, n], U32, name=f"words{j}", align_bytes=64)
-            nc.sync.dma_start(out=w[:].bitcast(I32), in_=words_hbm[:, c0 : c0 + n])
+        for j in range(V // BANK):
+            w = keep.tile([P, BANK], U32, name=f"words{j}", align_bytes=64)
+            nc.sync.dma_start(out=w[:].bitcast(I32), in_=words_hbm[:, j * BANK : (j + 1) * BANK])
             words.append(w)
         list1 = keep.tile([P, I // 16], U16, name="list1")
         nc.sync.dma_start(list1[:], offs)
         list2 = keep.tile([P, I // 16], U16, name="list2")
         nc.sync.dma_start(list2[:], offs2)
-        sw1_t = keep.tile([P, I], F32, name="sw1_t")
-        sw2_t = keep.tile([P, I], F32, name="sw2_t")
-        nc.sync.dma_start(out=sw2_t[:], in_=sw2[0].partition_broadcast(P))
-        nc.sync.dma_start(out=sw1_t[:], in_=sw[0].partition_broadcast(P))
+        sw1_c = keep.tile([P, 4], F32, name="sw1_c")
+        sw2_c = keep.tile([P, 4], F32, name="sw2_c")
+        nc.sync.dma_start(out=sw2_c[:], in_=sw2[0].rearrange("(p t) -> p t", t=4))
+        nc.sync.dma_start(out=sw1_c[:], in_=sw[0].rearrange("(p t) -> p t", t=4))
         beta_t = keep.tile([P, 1], F32, name="beta_t")
         saved_t = keep.tile([P, 1], F32, name="saved_t")
         nc.sync.dma_start(out=beta_t[:], in_=beta)
@@ -70,19 +70,14 @@ def tile_attend_bodds_heads_kernel(tc, hid, voc_words, voc_scales, sw, sw2, save
         make_identity(nc, ident[:])
 
 
-        hid_bf = keep.tile([P, Q, 4], BF16, name="hid_bf", tag="hid_bf_then_win1", align_bytes=64)
+        hid_bf = keep.tile([P, Q, 4], BF16, name="hid_bf", align_bytes=64)
         nc.vector.tensor_copy(out=hid_bf[:], in_=hid_raw[:].rearrange("p t q -> p q t"))
         hid_codes = keep.tile([P, Q], U32, name="hid_codes", align_bytes=64)
         hid_scales = keep.tile([P, Q], U8, name="hid_scales", align_bytes=64)
         nc.vector.quantize_mx(out=hid_codes[:].bitcast(FP8X4), scales=hid_scales[:], in_=hid_bf[:].rearrange("p q t -> p (q t)"))
-        win1 = keep.tile([P, V], F32, name="win1", tag="hid_bf_then_win1", align_bytes=64)
-        nc.gpsimd.memset(win1[:], 0.0)
 
         a = keep.tile([P, V], F32, name="a")
-        piece_max = keep.tile([P, 8], F32, name="piece_max")
-        early_max = keep.tile([P, 1], F32, name="early_max")
-        row_max = keep.tile([P, 1], F32, name="row_max")
-        last = len(SCORE_PIECES) - 1
+        piece_max = [keep.tile([P, 1], F32, name=f"piece_max{j}") for j in range(len(SCORE_PIECES))]
         for j, (c0, n) in enumerate(SCORE_PIECES):
             bank = psum.tile([P, BANK], F32, name=f"score{j}", tag=f"bank{j}")
             k = 4 * (c0 // BANK)
@@ -90,18 +85,18 @@ def tile_attend_bodds_heads_kernel(tc, hid, voc_words, voc_scales, sw, sw2, save
                 out=bank[:, 0:n],
                 lhsT=hid_codes[:].bitcast(FP8X4),
                 lhsT_scale=hid_scales[:],
-                rhs=words[j][:].bitcast(FP8X4),
+                rhs=words[c0 // BANK][:, c0 % BANK : c0 % BANK + n].bitcast(FP8X4),
                 rhs_scale=planes[k:P, c0 % BANK : c0 % BANK + n],
                 start=True,
                 stop=True,
             )
-            if j < last:
-                nc.vector.tensor_scalar(out=a[:, c0 : c0 + n], in0=bank[:, 0:n], scalar1=1.0, scalar2=None, op0=ALU.mult, op1=ALU.max, accum_out=piece_max[:, j : j + 1])
-            else:
-                nc.vector.tensor_reduce(out=early_max[:], in_=piece_max[:, 0:last], axis=AX.X, op=ALU.max)
-                nc.vector.tensor_scalar(out=a[:, c0 : c0 + n], in0=bank[:, 0:n], scalar1=1.0, scalar2=early_max[:], op0=ALU.mult, op1=ALU.max, accum_out=row_max[:])
+            nc.vector.tensor_scalar(out=a[:, c0 : c0 + n], in0=bank[:, 0:n], scalar1=1.0, scalar2=(piece_max[j - 2][:] if j >= 2 else None), op0=ALU.mult, op1=ALU.max, accum_out=piece_max[j][:])
         neg_max = keep.tile([P, 1], F32, name="neg_max")
-        nc.scalar.activation(out=neg_max[:], in_=row_max[:], func=ACT.Copy, scale=-1.0)
+        neg_odd = keep.tile([P, 1], F32, name="neg_odd")
+        excess = keep.tile([P, 1], F32, name="excess")
+        nc.scalar.activation(out=neg_odd[:], in_=piece_max[-2][:], func=ACT.Copy, scale=-1.0)
+        nc.scalar.activation(out=excess[:], in_=piece_max[-1][:], func=ACT.Relu, bias=neg_odd[:])
+        nc.scalar.activation(out=neg_max[:], in_=excess[:], func=ACT.Identity, scale=-1.0, bias=neg_odd[:])
 
         neg_beta = keep.tile([P, 1], F32, name="neg_beta")
         beta_saved = keep.tile([P, 1], F32, name="beta_saved")
@@ -111,6 +106,11 @@ def tile_attend_bodds_heads_kernel(tc, hid, voc_words, voc_scales, sw, sw2, save
         nc.scalar.activation(out=beta256[:, 0:1], in_=beta_t[:], func=ACT.Copy, scale=256.0)
         nc.scalar.activation(out=beta256[:, 1:2], in_=beta_t[:], func=ACT.Copy, scale=-256.0)
 
+        sw1_b = psum.tile([P, 4, P], F32, name="sw1_b", tag="bank3")
+        sw2_b = psum.tile([P, 4, P], F32, name="sw2_b", tag="bank4")
+        for spread, cols in ((sw1_b, sw1_c), (sw2_b, sw2_c)):
+            for t in range(4):
+                nc.tensor.transpose(spread[:, t, :], cols[:, t : t + 1].to_broadcast([P, P]), ident[:])
         nturn = len(TURNED)
         turned = []
         for b, (c0, n) in enumerate(TURNED):
@@ -121,39 +121,48 @@ def tile_attend_bodds_heads_kernel(tc, hid, voc_words, voc_scales, sw, sw2, save
                 o = c0 % BANK + i * P
                 nc.tensor.matmul(t[:, i * P : (i + 1) * P], lhsT=src[:, o : o + P], rhs=ident[:], start=(i == 0), stop=False, is_transpose=True)
 
-        px2 = keep.tile([P, I], F32, name="px2")
+        def by4(ap):
+            return ap.rearrange("p (n t) -> p n t", t=4)
+
+        g1 = keep.tile([P, I], F32, name="g1", tag="g1_then_win1")
         g2 = keep.tile([P, I], F32, name="g2")
+        px1 = keep.tile([P, I], F32, name="px1")
+        px2 = keep.tile([P, I], F32, name="px2")
+        nc.vector.tensor_copy(out=g1[:], in_=a[:].indirect(list1[:]))
+        nc.scalar.activation(out=px1[:], in_=g1[:], func=ACT.Exp, bias=neg_max[:])
         nc.vector.tensor_copy(out=g2[:], in_=a[:].indirect(list2[:]))
         nc.scalar.activation(out=px2[:], in_=g2[:], func=ACT.Exp, bias=neg_max[:])
-        g1 = keep.tile([P, I], F32, name="g1")
-        nc.vector.tensor_copy(out=g1[:], in_=a[:].indirect(list1[:]))
-        px1 = keep.tile([P, I], F32, name="px1")
-        nc.scalar.activation(out=px1[:], in_=g1[:], func=ACT.Exp, bias=neg_max[:])
+        win1 = keep.tile([P, V], F32, name="win1", tag="g1_then_win1")
+        nc.gpsimd.memset(win1[:], 0.0)
         sum1 = keep.tile([P, 1], F32, name="sum1")
         sum2 = keep.tile([P, 1], F32, name="sum2")
         w1 = keep.tile([P, I], F32, name="w1")
         w2 = keep.tile([P, I], F32, name="w2")
         inv1 = keep.tile([P, 1], F32, name="inv1")
         inv2 = keep.tile([P, 1], F32, name="inv2")
-        nc.vector.scalar_tensor_tensor(out=w2[:], in0=px2[:], scalar=1.0, in1=sw2_t[:], op0=ALU.mult, op1=ALU.mult, accum_out=sum2[:])
-        nc.vector.scalar_tensor_tensor(out=w1[:], in0=px1[:], scalar=1.0, in1=sw1_t[:], op0=ALU.mult, op1=ALU.mult, accum_out=sum1[:])
+        nc.vector.scalar_tensor_tensor(out=by4(w1[:]), in0=by4(px1[:]), scalar=1.0, in1=sw1_b[:].rearrange("p t n -> p n t"), op0=ALU.mult, op1=ALU.mult, accum_out=sum1[:])
+        nc.vector.reciprocal(out=inv1[:], in_=sum1[:])
+        nc.vector.scalar_tensor_tensor(out=by4(w2[:]), in0=by4(px2[:]), scalar=1.0, in1=sw2_b[:].rearrange("p t n -> p n t"), op0=ALU.mult, op1=ALU.mult, accum_out=sum2[:])
         nc.vector.reciprocal(out=inv2[:], in_=sum2[:])
         nc.vector.tensor_copy(out=win2[:].indirect(list2[:]), in_=w2[:])
-        nc.vector.reciprocal(out=inv1[:], in_=sum1[:])
         nc.vector.tensor_copy(out=win1[:].indirect(list1[:]), in_=w1[:])
 
-        log_odds = keep.tile([P, 1], F32, name="log_odds")
-        nc.scalar.activation(out=log_odds[:], in_=sum1[:], func=ACT.Ln, scale=inv2[:])
-        pre2 = keep.tile([P, 1], F32, name="pre2")
-        nc.scalar.activation(out=pre2[:], in_=inv2[:], func=ACT.Copy, scale=beta256[:, 1:2])
+        ln1 = keep.tile([P, 1], F32, name="ln1")
+        ln2 = keep.tile([P, 1], F32, name="ln2")
+        shift = keep.tile([P, 1], F32, name="shift")
+        nc.scalar.activation(out=ln1[:], in_=sum1[:], func=ACT.Ln, scale=2.0**32)
+        nc.scalar.activation(out=shift[:], in_=ln1[:], func=ACT.Identity, scale=neg_beta[:], bias=beta_saved[:])
+        nc.scalar.activation(out=ln2[:], in_=sum2[:], func=ACT.Ln, scale=2.0**32)
         sig = keep.tile([P, 1], F32, name="sig")
-        nc.scalar.activation(out=sig[:], in_=log_odds[:], func=ACT.Sigmoid, scale=neg_beta[:], bias=beta_saved[:])
-        coef2 = keep.tile([P, 1], F32, name="coef2")
-        nc.scalar.activation(out=coef2[:], in_=pre2[:], func=ACT.Copy, scale=sig[:])
+        nc.scalar.activation(out=sig[:], in_=ln2[:], func=ACT.Sigmoid, scale=beta_t[:], bias=shift[:])
+        ddl256 = keep.tile([P, 2], F32, name="ddl256")
+        nc.scalar.activation(out=ddl256[:], in_=beta256[:], func=ACT.Copy, scale=sig[:])
         coef1 = keep.tile([P, 1], F32, name="coef1")
-        nc.vector.tensor_scalar(out=coef1[:], in0=inv1[:], scalar1=sig[:], scalar2=beta256[:, 0:1], op0=ALU.mult, op1=ALU.mult)
+        coef2 = keep.tile([P, 1], F32, name="coef2")
+        nc.scalar.activation(out=coef1[:], in_=inv1[:], func=ACT.Copy, scale=ddl256[:, 0:1])
+        nc.scalar.activation(out=coef2[:], in_=inv2[:], func=ACT.Copy, scale=ddl256[:, 1:2])
 
-        scaled = [keep.tile([P, BANK], F32, name=f"scaled{b}", tag=f"old_then_scaled{(3, 2, 1, 4)[b]}") for b in range(nturn)]
+        scaled = [keep.tile([P, BANK], F32, name=f"scaled{b}", tag=f"old_then_scaled{(2, 1, 0, 4)[b]}") for b in range(nturn)]
         summed = [keep.tile([P, BANK], F32, name=f"summed{b}") for b in range(nturn)]
         back = [psum.tile([P, BANK], F32, name=f"back{b}", tag=f"bank{b + 1}") for b in range(nturn)]
 
@@ -176,14 +185,9 @@ def tile_attend_bodds_heads_kernel(tc, hid, voc_words, voc_scales, sw, sw2, save
             turn_back(b)
 
         part = keep.tile([P, DIRECT], F32, name="part")
-        nc.vector.scalar_tensor_tensor(out=part[:], in0=win2[:, 0:DIRECT], scalar=coef2[:], in1=old_t[0][:, 0:DIRECT], op0=ALU.mult, op1=ALU.add)
+        nc.vector.scalar_tensor_tensor(out=part[:], in0=win2[:, V - DIRECT : V], scalar=coef2[:], in1=old_t[3][:, BANK - DIRECT : BANK], op0=ALU.mult, op1=ALU.add)
         for j, (c0, n) in enumerate(OUT_PIECES):
             res = keep.tile([P, n], F32, name=f"res{j}")
-            if c0 < DIRECT:
-                other = part[:, c0 : c0 + n]
-            else:
-                b = c0 // BANK
-                off = c0 - TURNED[b][0]
-                other = back[b][:, off : off + n]
+            other = part[:] if j == 0 else back[j - 1][:, 0:n]
             nc.vector.scalar_tensor_tensor(out=res[:], in0=win1[:, c0 : c0 + n], scalar=coef1[:], in1=other, op0=ALU.mult, op1=ALU.add)
             nc.sync.dma_start(out=out[:, c0 : c0 + n], in_=res[:])

@@ -20,9 +20,8 @@ AX = mybir.AxisListType
 P = 128
 BANK = 512
 SCORE_PIECES = [(0, 256), (256, 256), (512, 512), (1024, 512), (1536, 512)]
-DIRECT = 384
-TURNED = [(0, 512), (512, 512), (1024, 512), (1536, 128)]
-OUT_PIECES = [(V - DIRECT, DIRECT)] + TURNED
+TURNED = [(0, 512), (512, 512), (1024, 256)]
+ON_GPSIMD = [(1280, 384), (1664, 384)]
 
 
 def tile_attend_bodds_heads_kernel(tc, hid, voc_words, voc_scales, sw, sw2, saved, beta, old, offs, offs2, out):
@@ -59,9 +58,9 @@ def tile_attend_bodds_heads_kernel(tc, hid, voc_words, voc_scales, sw, sw2, save
         nc.sync.dma_start(out=beta_t[:], in_=beta)
         nc.sync.dma_start(out=saved_t[:], in_=saved)
         old_t = []
-        for b in range(V // BANK):
-            o = keep.tile([P, BANK], F32, name=f"old{b}", tag=f"old_then_scaled{b}")
-            nc.sync.dma_start(out=o[:], in_=old[:, b * BANK : (b + 1) * BANK])
+        for b, (c0, n) in enumerate(TURNED + ON_GPSIMD):
+            o = keep.tile([P, n], F32, name=f"old{b}", tag=f"old_then_scaled{b}")
+            nc.sync.dma_start(out=o[:], in_=old[:, c0 : c0 + n])
             old_t.append(o)
 
         win2 = keep.tile([P, V], F32, name="win2")
@@ -114,12 +113,10 @@ def tile_attend_bodds_heads_kernel(tc, hid, voc_words, voc_scales, sw, sw2, save
         nturn = len(TURNED)
         turned = []
         for b, (c0, n) in enumerate(TURNED):
-            t = psum.tile([P, BANK], F32, name=f"turned{b}", tag=f"bank{(5 + b) % 8}")
+            t = psum.tile([P, BANK], F32, name=f"turned{b}", tag=f"bank{5 + b}")
             turned.append(t)
-            src = old_t[c0 // BANK]
             for i in range(n // P):
-                o = c0 % BANK + i * P
-                nc.tensor.matmul(t[:, i * P : (i + 1) * P], lhsT=src[:, o : o + P], rhs=ident[:], start=(i == 0), stop=False, is_transpose=True)
+                nc.tensor.matmul(t[:, i * P : (i + 1) * P], lhsT=old_t[b][:, i * P : (i + 1) * P], rhs=ident[:], start=(i == 0), stop=False, is_transpose=True)
 
         def by4(ap):
             return ap.rearrange("p (n t) -> p n t", t=4)
@@ -162,9 +159,9 @@ def tile_attend_bodds_heads_kernel(tc, hid, voc_words, voc_scales, sw, sw2, save
         nc.scalar.activation(out=coef1[:], in_=inv1[:], func=ACT.Copy, scale=ddl256[:, 0:1])
         nc.scalar.activation(out=coef2[:], in_=inv2[:], func=ACT.Copy, scale=ddl256[:, 1:2])
 
-        scaled = [keep.tile([P, BANK], F32, name=f"scaled{b}", tag=f"old_then_scaled{(2, 1, 0, 4)[b]}") for b in range(nturn)]
-        summed = [keep.tile([P, BANK], F32, name=f"summed{b}") for b in range(nturn)]
-        back = [psum.tile([P, BANK], F32, name=f"back{b}", tag=f"bank{b + 1}") for b in range(nturn)]
+        scaled = [keep.tile([P, BANK], F32, name=f"scaled{b}", tag=f"old_then_scaled{nturn - 1 - b}") for b in range(nturn)]
+        summed = [keep.tile([P, BANK], F32, name=f"summed{b}", tag=f"summed{b}") for b in range(nturn)]
+        back = [psum.tile([P, BANK], F32, name=f"back{b}", tag=f"bank{b}") for b in range(nturn)]
 
         def scale_and_add(b):
             c0, n = TURNED[b]
@@ -184,10 +181,16 @@ def tile_attend_bodds_heads_kernel(tc, hid, voc_words, voc_scales, sw, sw2, save
                 scale_and_add(b + 1)
             turn_back(b)
 
-        part = keep.tile([P, DIRECT], F32, name="part")
-        nc.vector.scalar_tensor_tensor(out=part[:], in0=win2[:, V - DIRECT : V], scalar=coef2[:], in1=old_t[3][:, BANK - DIRECT : BANK], op0=ALU.mult, op1=ALU.add)
-        for j, (c0, n) in enumerate(OUT_PIECES):
+        parts = []
+        for j, (c0, n) in enumerate(ON_GPSIMD):
+            scaled_g = keep.tile([P, n], F32, name=f"scaled_g{j}")
+            part = keep.tile([P, n], F32, name=f"part{j}")
+            nc.gpsimd.tensor_scalar(out=scaled_g[:], in0=win2[:, c0 : c0 + n], scalar1=coef2[:], scalar2=0.0, op0=ALU.mult, op1=ALU.add)
+            nc.gpsimd.tensor_tensor(out=part[:], in0=scaled_g[:], in1=old_t[nturn + j][:], op=ALU.add)
+            parts.append(part[:])
+
+        pieces = [(ON_GPSIMD[0], parts[0]), (TURNED[0], back[0][:]), (ON_GPSIMD[1], parts[1]), (TURNED[1], back[1][:]), (TURNED[2], back[2][:, 0 : TURNED[2][1]])]
+        for j, ((c0, n), other) in enumerate(pieces):
             res = keep.tile([P, n], F32, name=f"res{j}")
-            other = part[:] if j == 0 else back[j - 1][:, 0:n]
             nc.vector.scalar_tensor_tensor(out=res[:], in0=win1[:, c0 : c0 + n], scalar=coef1[:], in1=other, op0=ALU.mult, op1=ALU.add)
             nc.sync.dma_start(out=out[:, c0 : c0 + n], in_=res[:])

@@ -21,7 +21,7 @@ P = 128
 BANK = 512
 SCORE_PIECES = [(0, 256), (256, 256), (512, 512), (1024, 512), (1536, 512)]
 TURNED = [(0, 512), (512, 512), (1024, 256)]
-ON_GPSIMD = [(1280, 384), (1664, 384)]
+ON_GPSIMD = [(1280, 768)]
 
 
 def tile_attend_bodds_heads_kernel(tc, hid, voc_words, voc_scales, sw, sw2, saved, beta, old, offs, offs2, out):
@@ -98,12 +98,13 @@ def tile_attend_bodds_heads_kernel(tc, hid, voc_words, voc_scales, sw, sw2, save
         nc.scalar.activation(out=neg_max[:], in_=excess[:], func=ACT.Identity, scale=-1.0, bias=neg_odd[:])
 
         neg_beta = keep.tile([P, 1], F32, name="neg_beta")
-        beta_saved = keep.tile([P, 1], F32, name="beta_saved")
-        beta256 = keep.tile([P, 2], F32, name="beta256")
+        neg_beta256 = keep.tile([P, 1], F32, name="neg_beta256")
+        exp_saved = keep.tile([P, 1], F32, name="exp_saved")
         nc.scalar.activation(out=neg_beta[:], in_=beta_t[:], func=ACT.Copy, scale=-1.0)
-        nc.scalar.activation(out=beta_saved[:], in_=saved_t[:], func=ACT.Copy, scale=beta_t[:])
-        nc.scalar.activation(out=beta256[:, 0:1], in_=beta_t[:], func=ACT.Copy, scale=256.0)
-        nc.scalar.activation(out=beta256[:, 1:2], in_=beta_t[:], func=ACT.Copy, scale=-256.0)
+        nc.scalar.activation(out=neg_beta256[:], in_=beta_t[:], func=ACT.Copy, scale=-256.0)
+        nc.scalar.activation(out=exp_saved[:], in_=saved_t[:], func=ACT.Exp)
+        minus_one = keep.tile([P, 1], F32, name="minus_one")
+        nc.gpsimd.memset(minus_one[:], -1.0)
 
         sw1_b = psum.tile([P, 4, P], F32, name="sw1_b", tag="bank3")
         sw2_b = psum.tile([P, 4, P], F32, name="sw2_b", tag="bank4")
@@ -136,28 +137,28 @@ def tile_attend_bodds_heads_kernel(tc, hid, voc_words, voc_scales, sw, sw2, save
         w1 = keep.tile([P, I], F32, name="w1")
         w2 = keep.tile([P, I], F32, name="w2")
         inv1 = keep.tile([P, 1], F32, name="inv1")
-        inv2 = keep.tile([P, 1], F32, name="inv2")
         nc.vector.scalar_tensor_tensor(out=by4(w1[:]), in0=by4(px1[:]), scalar=1.0, in1=sw1_b[:].rearrange("p t n -> p n t"), op0=ALU.mult, op1=ALU.mult, accum_out=sum1[:])
         nc.vector.reciprocal(out=inv1[:], in_=sum1[:])
         nc.vector.scalar_tensor_tensor(out=by4(w2[:]), in0=by4(px2[:]), scalar=1.0, in1=sw2_b[:].rearrange("p t n -> p n t"), op0=ALU.mult, op1=ALU.mult, accum_out=sum2[:])
-        nc.vector.reciprocal(out=inv2[:], in_=sum2[:])
         nc.vector.tensor_copy(out=win2[:].indirect(list2[:]), in_=w2[:])
         nc.vector.tensor_copy(out=win1[:].indirect(list1[:]), in_=w1[:])
 
-        ln1 = keep.tile([P, 1], F32, name="ln1")
-        ln2 = keep.tile([P, 1], F32, name="ln2")
-        shift = keep.tile([P, 1], F32, name="shift")
-        nc.scalar.activation(out=ln1[:], in_=sum1[:], func=ACT.Ln, scale=2.0**32)
-        nc.scalar.activation(out=shift[:], in_=ln1[:], func=ACT.Identity, scale=neg_beta[:], bias=beta_saved[:])
-        nc.scalar.activation(out=ln2[:], in_=sum2[:], func=ACT.Ln, scale=2.0**32)
-        sig = keep.tile([P, 1], F32, name="sig")
-        nc.scalar.activation(out=sig[:], in_=ln2[:], func=ACT.Sigmoid, scale=beta_t[:], bias=shift[:])
-        ddl256 = keep.tile([P, 2], F32, name="ddl256")
-        nc.scalar.activation(out=ddl256[:], in_=beta256[:], func=ACT.Copy, scale=sig[:])
+        ratio = keep.tile([P, 1], F32, name="ratio")
+        neg_ratio = keep.tile([P, 1], F32, name="neg_ratio")
+        base = keep.tile([P, 1], F32, name="base")
+        odds = keep.tile([P, 1], F32, name="odds")
+        denom = keep.tile([P, 1], F32, name="denom")
+        sig_over_s2 = keep.tile([P, 1], F32, name="sig_over_s2")
+        nc.scalar.activation(out=ratio[:], in_=sum2[:], func=ACT.Copy, scale=inv1[:])
+        nc.scalar.activation(out=base[:], in_=ratio[:], func=ACT.Copy, scale=exp_saved[:])
+        nc.scalar.activation(out=neg_ratio[:], in_=ratio[:], func=ACT.Copy, scale=-1.0)
+        nc.gpsimd.tensor_tensor(out=odds[:], in0=base[:], in1=neg_beta[:], op=ALU.pow)
+        nc.gpsimd.tensor_scalar(out=denom[:], in0=odds[:], scalar1=1.0, scalar2=sum2[:], op0=ALU.add, op1=ALU.mult)
+        nc.gpsimd.tensor_tensor(out=sig_over_s2[:], in0=denom[:], in1=minus_one[:], op=ALU.pow)
         coef1 = keep.tile([P, 1], F32, name="coef1")
         coef2 = keep.tile([P, 1], F32, name="coef2")
-        nc.scalar.activation(out=coef1[:], in_=inv1[:], func=ACT.Copy, scale=ddl256[:, 0:1])
-        nc.scalar.activation(out=coef2[:], in_=inv2[:], func=ACT.Copy, scale=ddl256[:, 1:2])
+        nc.scalar.activation(out=coef2[:], in_=sig_over_s2[:], func=ACT.Copy, scale=neg_beta256[:])
+        nc.scalar.activation(out=coef1[:], in_=coef2[:], func=ACT.Copy, scale=neg_ratio[:])
 
         scaled = [keep.tile([P, BANK], F32, name=f"scaled{b}", tag=f"old_then_scaled{nturn - 1 - b}") for b in range(nturn)]
         summed = [keep.tile([P, BANK], F32, name=f"summed{b}", tag=f"summed{b}") for b in range(nturn)]
@@ -187,9 +188,9 @@ def tile_attend_bodds_heads_kernel(tc, hid, voc_words, voc_scales, sw, sw2, save
             part = keep.tile([P, n], F32, name=f"part{j}")
             nc.gpsimd.tensor_scalar(out=scaled_g[:], in0=win2[:, c0 : c0 + n], scalar1=coef2[:], scalar2=0.0, op0=ALU.mult, op1=ALU.add)
             nc.gpsimd.tensor_tensor(out=part[:], in0=scaled_g[:], in1=old_t[nturn + j][:], op=ALU.add)
-            parts.append(part[:])
+            parts.append(part)
 
-        pieces = [(ON_GPSIMD[0], parts[0]), (TURNED[0], back[0][:]), (ON_GPSIMD[1], parts[1]), (TURNED[1], back[1][:]), (TURNED[2], back[2][:, 0 : TURNED[2][1]])]
+        pieces = [((1280, 384), parts[0][:, 0:384]), ((1664, 384), parts[0][:, 384:768]), (TURNED[0], back[0][:]), (TURNED[1], back[1][:]), (TURNED[2], back[2][:, 0:256])]
         for j, ((c0, n), other) in enumerate(pieces):
             res = keep.tile([P, n], F32, name=f"res{j}")
             nc.vector.scalar_tensor_tensor(out=res[:], in0=win1[:, c0 : c0 + n], scalar=coef1[:], in1=other, op0=ALU.mult, op1=ALU.add)

from contextlib import ExitStack

import concourse.mybir as mybir
from concourse.masks import make_identity

D, V, Q, I = 512, 2048, 128, 512
FLOPS = 2 * D * V * Q

F32 = mybir.dt.float32
BF16 = mybir.dt.bfloat16
I32 = mybir.dt.int32
U32 = mybir.dt.uint32
U16 = mybir.dt.uint16
U8 = mybir.dt.uint8
FP8X4 = mybir.dt.float8_e4m3fn_x4
ALU = mybir.AluOpType
ACT = mybir.ActivationFunctionType
AX = mybir.AxisListType

P = 128
BANK = 512
SCORE_PIECES = [(0, 256), (256, 256), (512, 512), (1024, 512), (1536, 512)]
TURNED = [(0, 512), (512, 512), (1024, 256)]
ON_GPSIMD = [(1280, 768)]


def tile_attend_bodds_heads_kernel(tc, hid, voc_words, voc_scales, sw, sw2, saved, beta, old, offs, offs2, out):
    nc = tc.nc
    with ExitStack() as ctx:
        keep = ctx.enter_context(tc.tile_pool(name="keep", bufs=1))
        psum = ctx.enter_context(tc.psum_pool(name="psum", bufs=1))

        planes = keep.tile([P, BANK], U8, name="planes", align_bytes=64)
        nc.gpsimd.memset(planes[:].bitcast(I32), 0)
        hid_raw = keep.tile([P, 4, Q], F32, name="hid_raw")
        nc.sync.dma_start(out=hid_raw[:], in_=hid.rearrange("(p t) q -> p t q", t=4))
        for quad in range(4):
            nc.sync.dma_start(
                out=planes[32 * quad : 32 * quad + 16, :].bitcast(I32),
                in_=voc_scales[0, 4 * quad : 4 * quad + 4, :].bitcast(I32).rearrange("r (j c) -> j r c", j=4),
            )
        words_hbm = voc_words[0].rearrange("p n t -> p (n t)").bitcast(I32)
        words = []
        for j in range(V // BANK):
            w = keep.tile([P, BANK], U32, name=f"words{j}", align_bytes=64)
            nc.sync.dma_start(out=w[:].bitcast(I32), in_=words_hbm[:, j * BANK : (j + 1) * BANK])
            words.append(w)
        list1 = keep.tile([P, I // 16], U16, name="list1")
        nc.sync.dma_start(list1[:], offs)
        list2 = keep.tile([P, I // 16], U16, name="list2")
        nc.sync.dma_start(list2[:], offs2)
        sw1_c = keep.tile([P, 4], F32, name="sw1_c")
        sw2_c = keep.tile([P, 4], F32, name="sw2_c")
        nc.sync.dma_start(out=sw2_c[:], in_=sw2[0].rearrange("(p t) -> p t", t=4))
        nc.sync.dma_start(out=sw1_c[:], in_=sw[0].rearrange("(p t) -> p t", t=4))
        beta_t = keep.tile([P, 1], F32, name="beta_t")
        saved_t = keep.tile([P, 1], F32, name="saved_t")
        nc.sync.dma_start(out=beta_t[:], in_=beta)
        nc.sync.dma_start(out=saved_t[:], in_=saved)
        old_t = []
        for b, (c0, n) in enumerate(TURNED + ON_GPSIMD):
            o = keep.tile([P, n], F32, name=f"old{b}", tag=f"old_then_scaled{b}")
            nc.sync.dma_start(out=o[:], in_=old[:, c0 : c0 + n])
            old_t.append(o)

        win2 = keep.tile([P, V], F32, name="win2")
        nc.vector.memset(win2[:], 0.0)
        ident = keep.tile([P, P], F32, name="ident")
        make_identity(nc, ident[:])


        hid_bf = keep.tile([P, Q, 4], BF16, name="hid_bf", align_bytes=64)
        nc.vector.tensor_copy(out=hid_bf[:], in_=hid_raw[:].rearrange("p t q -> p q t"))
        hid_codes = keep.tile([P, Q], U32, name="hid_codes", align_bytes=64)
        hid_scales = keep.tile([P, Q], U8, name="hid_scales", align_bytes=64)
        nc.vector.quantize_mx(out=hid_codes[:].bitcast(FP8X4), scales=hid_scales[:], in_=hid_bf[:].rearrange("p q t -> p (q t)"))

        a = keep.tile([P, V], F32, name="a")
        piece_max = [keep.tile([P, 1], F32, name=f"piece_max{j}") for j in range(len(SCORE_PIECES))]
        for j, (c0, n) in enumerate(SCORE_PIECES):
            bank = psum.tile([P, BANK], F32, name=f"score{j}", tag=f"bank{j}")
            k = 4 * (c0 // BANK)
            nc.tensor.matmul_mx(
                out=bank[:, 0:n],
                lhsT=hid_codes[:].bitcast(FP8X4),
                lhsT_scale=hid_scales[:],
                rhs=words[c0 // BANK][:, c0 % BANK : c0 % BANK + n].bitcast(FP8X4),
                rhs_scale=planes[k:P, c0 % BANK : c0 % BANK + n],
                start=True,
                stop=True,
            )
            nc.vector.tensor_scalar(out=a[:, c0 : c0 + n], in0=bank[:, 0:n], scalar1=1.0, scalar2=(piece_max[j - 2][:] if j >= 2 else None), op0=ALU.mult, op1=ALU.max, accum_out=piece_max[j][:])
        neg_max = keep.tile([P, 1], F32, name="neg_max")
        neg_odd = keep.tile([P, 1], F32, name="neg_odd")
        excess = keep.tile([P, 1], F32, name="excess")
        nc.scalar.activation(out=neg_odd[:], in_=piece_max[-2][:], func=ACT.Copy, scale=-1.0)
        nc.scalar.activation(out=excess[:], in_=piece_max[-1][:], func=ACT.Relu, bias=neg_odd[:])
        nc.scalar.activation(out=neg_max[:], in_=excess[:], func=ACT.Identity, scale=-1.0, bias=neg_odd[:])

        neg_beta = keep.tile([P, 1], F32, name="neg_beta")
        neg_beta256 = keep.tile([P, 1], F32, name="neg_beta256")
        exp_saved = keep.tile([P, 1], F32, name="exp_saved")
        nc.scalar.activation(out=neg_beta[:], in_=beta_t[:], func=ACT.Copy, scale=-1.0)
        nc.scalar.activation(out=neg_beta256[:], in_=beta_t[:], func=ACT.Copy, scale=-256.0)
        nc.scalar.activation(out=exp_saved[:], in_=saved_t[:], func=ACT.Exp)
        minus_one = keep.tile([P, 1], F32, name="minus_one")
        nc.gpsimd.memset(minus_one[:], -1.0)

        sw1_b = psum.tile([P, 4, P], F32, name="sw1_b", tag="bank3")
        sw2_b = psum.tile([P, 4, P], F32, name="sw2_b", tag="bank4")
        for spread, cols in ((sw1_b, sw1_c), (sw2_b, sw2_c)):
            for t in range(4):
                nc.tensor.transpose(spread[:, t, :], cols[:, t : t + 1].to_broadcast([P, P]), ident[:])
        nturn = len(TURNED)
        turned = []
        for b, (c0, n) in enumerate(TURNED):
            t = psum.tile([P, BANK], F32, name=f"turned{b}", tag=f"bank{5 + b}")
            turned.append(t)
            for i in range(n // P):
                nc.tensor.matmul(t[:, i * P : (i + 1) * P], lhsT=old_t[b][:, i * P : (i + 1) * P], rhs=ident[:], start=(i == 0), stop=False, is_transpose=True)

        def by4(ap):
            return ap.rearrange("p (n t) -> p n t", t=4)

        g1 = keep.tile([P, I], F32, name="g1", tag="g1_then_win1")
        g2 = keep.tile([P, I], F32, name="g2")
        px1 = keep.tile([P, I], F32, name="px1")
        px2 = keep.tile([P, I], F32, name="px2")
        nc.vector.tensor_copy(out=g1[:], in_=a[:].indirect(list1[:]))
        nc.scalar.activation(out=px1[:], in_=g1[:], func=ACT.Exp, bias=neg_max[:])
        nc.vector.tensor_copy(out=g2[:], in_=a[:].indirect(list2[:]))
        nc.scalar.activation(out=px2[:], in_=g2[:], func=ACT.Exp, bias=neg_max[:])
        win1 = keep.tile([P, V], F32, name="win1", tag="g1_then_win1")
        nc.gpsimd.memset(win1[:], 0.0)
        sum1 = keep.tile([P, 1], F32, name="sum1")
        sum2 = keep.tile([P, 1], F32, name="sum2")
        w1 = keep.tile([P, I], F32, name="w1")
        w2 = keep.tile([P, I], F32, name="w2")
        inv1 = keep.tile([P, 1], F32, name="inv1")
        nc.vector.scalar_tensor_tensor(out=by4(w1[:]), in0=by4(px1[:]), scalar=1.0, in1=sw1_b[:].rearrange("p t n -> p n t"), op0=ALU.mult, op1=ALU.mult, accum_out=sum1[:])
        nc.vector.reciprocal(out=inv1[:], in_=sum1[:])
        nc.vector.scalar_tensor_tensor(out=by4(w2[:]), in0=by4(px2[:]), scalar=1.0, in1=sw2_b[:].rearrange("p t n -> p n t"), op0=ALU.mult, op1=ALU.mult, accum_out=sum2[:])
        nc.vector.tensor_copy(out=win2[:].indirect(list2[:]), in_=w2[:])
        nc.vector.tensor_copy(out=win1[:].indirect(list1[:]), in_=w1[:])

        ratio = keep.tile([P, 1], F32, name="ratio")
        neg_ratio = keep.tile([P, 1], F32, name="neg_ratio")
        base = keep.tile([P, 1], F32, name="base")
        odds = keep.tile([P, 1], F32, name="odds")
        denom = keep.tile([P, 1], F32, name="denom")
        sig_over_s2 = keep.tile([P, 1], F32, name="sig_over_s2")
        nc.scalar.activation(out=ratio[:], in_=sum2[:], func=ACT.Copy, scale=inv1[:])
        nc.scalar.activation(out=base[:], in_=ratio[:], func=ACT.Copy, scale=exp_saved[:])
        nc.scalar.activation(out=neg_ratio[:], in_=ratio[:], func=ACT.Copy, scale=-1.0)
        nc.gpsimd.tensor_tensor(out=odds[:], in0=base[:], in1=neg_beta[:], op=ALU.pow)
        nc.gpsimd.tensor_scalar(out=denom[:], in0=odds[:], scalar1=1.0, scalar2=sum2[:], op0=ALU.add, op1=ALU.mult)
        nc.gpsimd.tensor_tensor(out=sig_over_s2[:], in0=denom[:], in1=minus_one[:], op=ALU.pow)
        coef1 = keep.tile([P, 1], F32, name="coef1")
        coef2 = keep.tile([P, 1], F32, name="coef2")
        nc.scalar.activation(out=coef2[:], in_=sig_over_s2[:], func=ACT.Copy, scale=neg_beta256[:])
        nc.scalar.activation(out=coef1[:], in_=coef2[:], func=ACT.Copy, scale=neg_ratio[:])

        scaled = [keep.tile([P, BANK], F32, name=f"scaled{b}", tag=f"old_then_scaled{nturn - 1 - b}") for b in range(nturn)]
        summed = [keep.tile([P, BANK], F32, name=f"summed{b}", tag=f"summed{b}") for b in range(nturn)]
        back = [psum.tile([P, BANK], F32, name=f"back{b}", tag=f"bank{b}") for b in range(nturn)]

        def scale_and_add(b):
            c0, n = TURNED[b]
            nc.scalar.activation(out=scaled[b][:, 0:n], in_=win2[:, c0 : c0 + n], func=ACT.Copy, scale=coef2[:])
            for i in range(n // P):
                nc.tensor.matmul(turned[b][:, i * P : (i + 1) * P], lhsT=scaled[b][:, i * P : (i + 1) * P], rhs=ident[:], start=False, stop=(i == n // P - 1), is_transpose=True)

        def turn_back(b):
            c0, n = TURNED[b]
            nc.scalar.copy(out=summed[b][:, 0:n], in_=turned[b][:, 0:n])
            for i in range(n // P):
                nc.tensor.transpose(back[b][:, i * P : (i + 1) * P], summed[b][:, i * P : (i + 1) * P], ident[:])

        scale_and_add(0)
        for b in range(nturn):
            if b + 1 < nturn:
                scale_and_add(b + 1)
            turn_back(b)

        parts = []
        for j, (c0, n) in enumerate(ON_GPSIMD):
            scaled_g = keep.tile([P, n], F32, name=f"scaled_g{j}")
            part = keep.tile([P, n], F32, name=f"part{j}")
            nc.gpsimd.tensor_scalar(out=scaled_g[:], in0=win2[:, c0 : c0 + n], scalar1=coef2[:], scalar2=0.0, op0=ALU.mult, op1=ALU.add)
            nc.gpsimd.tensor_tensor(out=part[:], in0=scaled_g[:], in1=old_t[nturn + j][:], op=ALU.add)
            parts.append(part)

        pieces = [((1280, 384), parts[0][:, 0:384]), ((1664, 384), parts[0][:, 384:768]), (TURNED[0], back[0][:]), (TURNED[1], back[1][:]), (TURNED[2], back[2][:, 0:256])]
        for j, ((c0, n), other) in enumerate(pieces):
            res = keep.tile([P, n], F32, name=f"res{j}")
            nc.vector.scalar_tensor_tensor(out=res[:], in0=win1[:, c0 : c0 + n], scalar=coef1[:], in1=other, op0=ALU.mult, op1=ALU.add)
            nc.sync.dma_start(out=out[:, c0 : c0 + n], in_=res[:])
